import numpy as np
import ml_dtypes


def mxq(x, axis, fmt="e4m3"):
    dtype, down = {"e4m3": (ml_dtypes.float8_e4m3fn, 7), "e5m2": (ml_dtypes.float8_e5m2, 14)}[fmt]
    v = np.moveaxis(np.asarray(x, np.float32).astype(ml_dtypes.bfloat16).astype(np.float64), axis, -1)
    blocks = v.reshape(v.shape[:-1] + (-1, 32))
    amax = np.abs(blocks).max(-1, keepdims=True)
    byte = np.maximum(np.where(amax > 0, np.frexp(amax)[1] - 1 + 127, 0) - down, 1)
    scale = np.exp2(byte - 127.0)
    codes = (blocks / scale).astype(np.float32).astype(dtype).astype(np.float64)
    return np.moveaxis((codes * scale).reshape(v.shape), -1, axis)


WIDE = False


def mx_kscale(k):
    if not WIDE:
        return np.ones(k)
    levels = np.array([10, -10, 5, -5, 0])
    if k % 512:
        return np.exp2(np.random.permutation(np.resize(levels, k // 32))).repeat(32)
    a = np.empty((k // 512, 16))
    for p in range(k // 512):
        a[p, :8] = np.random.permutation(np.resize(levels, 8))
        for g in range(8):
            far = levels[np.abs(levels - a[p, g]) >= 10]
            a[p, g + 8] = far[np.random.randint(len(far))]
    return np.exp2(a.ravel()).repeat(32)


def f64(x):
    return np.asarray(x).astype(np.float64)


def striped(idx):
    return np.tile(np.asarray(idx).reshape(-1, 16).T, (8, 1)).astype(np.uint16)


def unstriped(offs):
    return offs[:16].T.reshape(-1).astype(np.int64)


E2M1 = np.array([0.0, 0.5, 1.0, 1.5, 2.0, 3.0, 4.0, 6.0, -0.0, -0.5, -1.0, -1.5, -2.0, -3.0, -4.0, -6.0])


def pack_weight(w, fmt):
    k, n = w.shape
    w = f64(np.asarray(w, np.float32).astype(ml_dtypes.bfloat16)).reshape(k // 32, 32, n)
    amax = np.abs(w).max(1)
    if fmt == "e4m3":
        byte = np.frexp(amax)[1] - 1 + 127 - 7
    else:
        mant, ex = np.frexp(amax / 6.0)
        byte = np.where(mant > 0.5, ex, ex - 1) + 127
    byte = np.clip(np.where(amax > 0, byte, 1), 1, 254)
    scaled = (w * np.exp2(127.0 - byte)[:, None, :]).reshape(k, n).astype(np.float32)
    by_word = np.ascontiguousarray(scaled.reshape(k // 512, 128, 4, n).transpose(0, 1, 3, 2))
    if fmt == "e4m3":
        words = by_word.astype(ml_dtypes.float8_e4m3fn).view(np.uint8)
    else:
        c = by_word.astype(ml_dtypes.float4_e2m1fn).view(np.uint8) & 0xF
        words = (c[..., 0::2] | (c[..., 1::2] << 4)).reshape(k // 512, 128, 2 * n)
    return np.ascontiguousarray(words), np.ascontiguousarray(byte.astype(np.uint8).reshape(k // 512, 16, n))


def unpack_weight(words, scales, fmt):
    g, _, n = scales.shape
    words = np.ascontiguousarray(words).reshape(g, 128, n, -1)
    if fmt == "e4m3":
        vals = words.view(ml_dtypes.float8_e4m3fn).astype(np.float64)
    else:
        nib = np.empty((g, 128, n, 4), np.uint8)
        nib[..., 0::2] = words & 0xF
        nib[..., 1::2] = words >> 4
        vals = E2M1[nib]
    vals = vals * np.repeat(np.exp2(scales.astype(np.float64) - 127.0), 8, axis=1)[..., None]
    return vals.transpose(0, 1, 3, 2).reshape(g * 512, n)


D, E, T, I, U, Q = 512, 512, 1024, 512, 2048, 128


def setup_inputs():
    n = np.random.standard_normal
    idx = np.random.permutation(T)[:I]
    idx2 = np.random.permutation(U)[:I]
    fd = mx_kscale(D)
    fe = mx_kscale(E)
    cvalsp = pack_weight(n((E, T)) / fe[:, None], "e4m3")
    return {
        "query": (n((D, Q)) * 0.6 / np.sqrt(D) * fd[:, None]).astype(np.float32),
        "keys": (n((D, T)) / fd[:, None]).astype(np.float32),
        "gout": (n((E, Q)) * 1 / np.sqrt(E) * fe[:, None]).astype(np.float32),
        "cvals_words": cvalsp[0],
        "cvals_scales": cvalsp[1],
        "corr": (n((E, U)) / fe[:, None]).astype(np.float32),
        "us": (np.random.uniform(0.5, 2.0, (1, I))).astype(np.float32),
        "old": (0.5 * n((Q, T))).astype(np.float32),
        "offs": striped(idx),
        "offs2": striped(idx2),
    }


def reference(query, keys, gout, cvals_words, cvals_scales, corr, us, old, offs, offs2):
    idx = unstriped(offs)
    idx2 = unstriped(offs2)
    cvalsu = unpack_weight(cvals_words, cvals_scales, "e4m3")
    queryq = mxq(f64(query), 0, "e4m3")
    keysq = mxq(f64(keys), 0, "e4m3")
    a = queryq.T @ keysq
    m1 = np.max(a, axis=1, keepdims=True)
    p = np.exp(a - m1)
    z = np.sum(p, axis=1, keepdims=True)
    px = np.exp(a[:, idx] - m1)
    goutq = mxq(f64(gout), 0, "e4m3")
    c0 = goutq.T @ cvalsu
    corridx2q = mxq(f64(corr)[:, idx2], 0, "e4m3")
    c1 = goutq.T @ corridx2q
    dpx = 1.0 / z * c1 * f64(us)
    dz = (np.sum(p * c0, axis=1, keepdims=True) + np.sum(px * f64(us) * c1, axis=1, keepdims=True)) / np.square(z) * (-1.0)
    dp = 1.0 / z * c0 + dz
    e1 = dpx * px
    s1 = np.zeros((Q, T))
    s1[:, idx] = e1
    da = dp * p + s1
    y = da * 1024.0 + f64(old)
    return y

@@ -1,0 +1,229 @@
+from contextlib import ExitStack
+
+import concourse.mybir as mybir
+from concourse.masks import make_identity
+
+D, E, T, I, U, Q = 512, 512, 1024, 512, 2048, 128
+FLOPS = 2 * Q * (D * T + E * T + E * I)
+
+F32 = mybir.dt.float32
+BF16 = mybir.dt.bfloat16
+I32 = mybir.dt.int32
+U32 = mybir.dt.uint32
+U16 = mybir.dt.uint16
+U8 = mybir.dt.uint8
+FP8X4 = mybir.dt.float8_e4m3fn_x4
+ALU = mybir.AluOpType
+ACT = mybir.ActivationFunctionType
+AX = mybir.AxisListType
+
+P = 128
+PACK = 4
+BANK = 512
+HALVES = T // BANK
+BLOCKS = BANK // P
+KQ = 256
+SH = I // 2
+GRAD_SCALE = 1024.0
+
+
+def weave_views(raw, woven):
+    return (
+        woven.rearrange("p (c i) t -> p c t i", i=4),
+        raw.rearrange("p t (c i) -> p c t i", i=4),
+    )
+
+
+def quantize(nc, woven, codes, scales):
+    nc.vector.quantize_mx(out=codes.bitcast(FP8X4), scales=scales, in_=woven.rearrange("p w t -> p (w t)"))
+
+
+def mx(nc, out, lhs, lhs_scales, rhs, rhs_scales):
+    nc.tensor.matmul_mx(out=out, lhsT=lhs.bitcast(FP8X4), lhsT_scale=lhs_scales,
+                        rhs=rhs.bitcast(FP8X4), rhs_scale=rhs_scales, start=True, stop=True)
+
+
+def tile_attend_bvaluepatch_kernel(tc, query, keys, gout, cvals_words, cvals_scales, corr, us, old, offs, offs2, out):
+    nc = tc.nc
+    with ExitStack() as ctx:
+        sb = ctx.enter_context(tc.tile_pool(name="sb", bufs=1))
+        ps = ctx.enter_context(tc.psum_pool(name="ps", bufs=1))
+
+        def tile(name, shape, dtype):
+            return sb.tile(shape, dtype, name=name, align_bytes=64)
+
+        def bank(tag, name, shape):
+            return ps.tile(shape, F32, name=name, tag=tag)
+
+        idx = sb.tile([P, I // 16], U16, name="idx")
+        idx2 = sb.tile([P, I // 16], U16, name="idx2")
+
+        cv_scales = tile("cv_scales", [P, T], U8)
+        nc.gpsimd.memset(cv_scales[:].bitcast(U32), 0)
+        ident = tile("ident", [P, P], F32)
+        make_identity(nc, ident[:])
+        s1 = tile("s1", [P, T], F32)
+        nc.gpsimd.memset(s1[:], 0.0)
+
+        q_raw = tile("q_raw", [P, PACK, Q], F32)
+        nc.sync.dma_start(out=q_raw[:], in_=query.rearrange("(p t) q -> p t q", t=PACK))
+        keys_v = keys.rearrange("(p t) n -> p t n", t=PACK)
+        k_raw = [tile(f"k_raw{h}", [P, PACK, BANK], F32) for h in range(HALVES)]
+        for h in range(HALVES):
+            nc.sync.dma_start(out=k_raw[h][:], in_=keys_v[:, :, h * BANK:(h + 1) * BANK])
+        us_col = tile("us_col", [P, PACK], F32)
+        nc.scalar.dma_start(out=us_col[:], in_=us.rearrange("o (p j) -> (o p) j", j=PACK))
+        for g in range(4):
+            nc.scalar.dma_start(out=cv_scales[32 * g:32 * g + 4, :].bitcast(I32),
+                                in_=cvals_scales[0][4 * g:4 * g + 4, :].bitcast(I32))
+        nc.sync.dma_start(idx[:], offs)
+        nc.sync.dma_start(idx2[:], offs2)
+        g_raw = tile("g_raw", [P, PACK, Q], F32)
+        nc.sync.dma_start(out=g_raw[:], in_=gout.rearrange("(p t) q -> p t q", t=PACK))
+        cv_codes = tile("cv_codes", [P, T], U32)
+        nc.sync.dma_start(out=cv_codes[:].bitcast(I32),
+                          in_=cvals_words[0].rearrange("p n t -> p (n t)").bitcast(I32))
+        corr_v = corr.rearrange("(p t) u -> p t u", t=PACK)
+        plane = [tile(f"plane{t}", [P, U], F32) for t in range(PACK)]
+        for t in range(PACK):
+            nc.sync.dma_start(out=plane[t][:], in_=corr_v[:, t, :])
+        old_sb = [tile(f"old{h}", [P, BANK], F32) for h in range(HALVES)]
+        for h in range(HALVES):
+            nc.sync.dma_start(out=old_sb[h][:], in_=old[:, h * BANK:(h + 1) * BANK])
+
+        q_w = tile("q_w", [P, Q, PACK], BF16)
+        dst, src = weave_views(q_raw[:], q_w[:])
+        nc.scalar.activation(out=dst, in_=src, func=ACT.Copy)
+        q_codes = tile("q_codes", [P, Q], U32)
+        q_scales = tile("q_scales", [P, Q], U8)
+        quantize(nc, q_w[:], q_codes[:], q_scales[:])
+
+        us_bank = bank("us", "us_bank", [P, PACK, P])
+        for j in range(PACK):
+            nc.tensor.transpose(us_bank[:, j, :], us_col[:, j:j + 1].to_broadcast([P, P]), ident[:])
+
+        a_sb = tile("a_sb", [P, T], F32)
+        neg_max = [tile(f"neg_max{h}", [P, 1], F32) for h in range(HALVES)]
+        for h in range(HALVES):
+            k_codes = tile(f"k_codes{h}", [P, BANK], U32)
+            k_scales = tile(f"k_scales{h}", [P, BANK], U8)
+            k_w = [tile(f"k_w{h}_{s}", [P, KQ, PACK], BF16) for s in range(2)]
+            for s in range(2):
+                dst, src = weave_views(k_raw[h][:, :, s * KQ:(s + 1) * KQ], k_w[s][:])
+                if s == 0:
+                    nc.vector.tensor_copy(out=dst, in_=src)
+                else:
+                    nc.scalar.activation(out=dst, in_=src, func=ACT.Copy)
+            for s in range(2):
+                quantize(nc, k_w[s][:], k_codes[:, s * KQ:(s + 1) * KQ], k_scales[:, s * KQ:(s + 1) * KQ])
+            a_bank = bank(f"a{h}", f"a_bank{h}", [P, BANK])
+            mx(nc, a_bank[:], q_codes[:], q_scales[:], k_codes[:], k_scales[:])
+            nc.vector.tensor_reduce(out=neg_max[h][:], in_=a_bank[:], axis=AX.X, op=ALU.max, negate=True)
+            nc.scalar.copy(out=a_sb[:, h * BANK:(h + 1) * BANK], in_=a_bank[:])
+        neg_m1 = tile("neg_m1", [P, 1], F32)
+        nc.vector.tensor_tensor(out=neg_m1[:], in0=neg_max[0][:], in1=neg_max[1][:], op=ALU.min)
+
+        p_sb = tile("p_sb", [P, T], F32)
+        z = tile("z", [P, 1], F32)
+        nc.scalar.activation(out=p_sb[:], in_=a_sb[:], func=ACT.Exp, bias=neg_m1[:], accum_out=z[:])
+
+        g_w = tile("g_w", [P, Q, PACK], BF16)
+        dst, src = weave_views(g_raw[:], g_w[:])
+        nc.scalar.activation(out=dst, in_=src, func=ACT.Copy)
+        g_codes = tile("g_codes", [P, Q], U32)
+        g_scales = tile("g_scales", [P, Q], U8)
+        quantize(nc, g_w[:], g_codes[:], g_scales[:])
+        c0_bank = [bank(f"c{h}", f"c0_bank{h}", [P, BANK]) for h in range(HALVES)]
+        for h in range(HALVES):
+            cols = slice(h * BANK, (h + 1) * BANK)
+            mx(nc, c0_bank[h][:], g_codes[:], g_scales[:], cv_codes[:, cols], cv_scales[:, cols])
+
+        ax = tile("ax", [P, I], F32)
+        nc.vector.tensor_copy(ax[:], a_sb[:].indirect(idx[:]))
+        px = tile("px", [P, I], F32)
+        nc.scalar.activation(out=px[:], in_=ax[:], func=ACT.Exp, bias=neg_m1[:])
+
+        rz = tile("rz", [P, 1], F32)
+        nc.vector.reciprocal(out=rz[:], in_=z[:])
+        rz_k = tile("rz_k", [P, 1], F32)
+        nc.vector.tensor_scalar(out=rz_k[:], in0=rz[:], scalar1=GRAD_SCALE, scalar2=None, op0=ALU.mult)
+        neg_rz_k = tile("neg_rz_k", [P, 1], F32)
+        nc.scalar.activation(out=neg_rz_k[:], in_=rz[:], func=ACT.Copy, scale=-GRAD_SCALE)
+        neg_rz = tile("neg_rz", [P, 1], F32)
+        nc.scalar.activation(out=neg_rz[:], in_=rz[:], func=ACT.Copy, scale=-1.0)
+
+        c_w = [tile(f"c_w{s}", [P, SH, PACK], BF16) for s in range(2)]
+        pair = tile("pair", [P, 2, I], BF16)
+        nc.vector.tensor_copy(pair[:, 0, :], plane[0][:].indirect(idx2[:]))
+
+        pc0 = tile("pc0", [P, T], F32)
+        pc0_sum = [tile(f"pc0_sum{h}", [P, 1], F32) for h in range(HALVES)]
+        for h in range(HALVES):
+            cols = slice(h * BANK, (h + 1) * BANK)
+            nc.vector.scalar_tensor_tensor(out=pc0[:, cols], in0=c0_bank[h][:], scalar=rz_k[:], in1=p_sb[:, cols],
+                                           op0=ALU.mult, op1=ALU.mult, accum_out=pc0_sum[h][:])
+        nc.vector.tensor_copy(pair[:, 1, :], plane[1][:].indirect(idx2[:]))
+        w = tile("w", [P, I], F32)
+        nc.vector.scalar_tensor_tensor(out=w[:].rearrange("p (n j) -> p n j", j=PACK),
+                                       in0=px[:].rearrange("p (n j) -> p n j", j=PACK), scalar=rz[:],
+                                       in1=us_bank[:].rearrange("p j n -> p n j"), op0=ALU.mult, op1=ALU.mult)
+        for s in range(2):
+            nc.scalar.copy(out=c_w[s][:, :, 0:2],
+                           in_=pair[:, :, s * SH:(s + 1) * SH].rearrange("p t n -> p n t"))
+
+        dz_a = tile("dz_a", [P, 1], F32)
+        nc.scalar.activation(out=dz_a[:], in_=pc0_sum[0][:], func=ACT.Copy, scale=neg_rz[:])
+        dz_b = tile("dz_b", [P, 1], F32)
+        nc.scalar.activation(out=dz_b[:], in_=pc0_sum[1][:], func=ACT.Identity, scale=neg_rz[:], bias=dz_a[:])
+
+        vt_bank = [bank(f"a{h}", f"vt_bank{h}", [P, BLOCKS, P]) for h in range(HALVES)]
+
+        def add_turned(h, src_ap, first, last):
+            for b in range(BLOCKS):
+                nc.tensor.matmul(vt_bank[h][:, b, :], lhsT=src_ap[:, b * P:(b + 1) * P], rhs=ident[:], is_transpose=True,
+                                 start=(first and b == 0), stop=(last and b == BLOCKS - 1))
+
+        for h in range(HALVES):
+            add_turned(h, pc0[:, h * BANK:(h + 1) * BANK], True, False)
+
+        for t in range(2, PACK):
+            for s in range(2):
+                nc.vector.tensor_copy(c_w[s][:, :, t], plane[t][:].indirect(idx2[:, s * (SH // 16):(s + 1) * (SH // 16)]))
+        for h in range(HALVES):
+            add_turned(h, old_sb[h][:], False, False)
+
+        c_codes = [tile(f"c_codes{s}", [P, SH], U32) for s in range(2)]
+        c_scales = [tile(f"c_scales{s}", [P, SH], U8) for s in range(2)]
+        c1_bank = [bank(f"e{s}", f"c1_bank{s}", [P, SH]) for s in range(2)]
+        for s in range(2):
+            quantize(nc, c_w[s][:], c_codes[s][:], c_scales[s][:])
+            mx(nc, c1_bank[s][:], g_codes[:], g_scales[:], c_codes[s][:], c_scales[s][:])
+
+        e1 = tile("e1", [P, I], F32)
+        e1_sum = [tile(f"e1_sum{s}", [P, 1], F32) for s in range(2)]
+        for s in range(2):
+            cols = slice(s * SH, (s + 1) * SH)
+            nc.vector.scalar_tensor_tensor(out=e1[:, cols], in0=c1_bank[s][:], scalar=1.0, in1=w[:, cols],
+                                           op0=ALU.mult, op1=ALU.mult, accum_out=e1_sum[s][:])
+        nc.vector.tensor_copy(s1[:].indirect(idx[:]), e1[:])
+
+        dz_c = tile("dz_c", [P, 1], F32)
+        nc.scalar.activation(out=dz_c[:], in_=e1_sum[0][:], func=ACT.Identity, scale=neg_rz_k[:], bias=dz_b[:])
+        dz_k = tile("dz_k", [P, 1], F32)
+        nc.scalar.activation(out=dz_k[:], in_=e1_sum[1][:], func=ACT.Identity, scale=neg_rz_k[:], bias=dz_c[:])
+
+        p_dz = [tile(f"p_dz{h}", [P, BANK], F32) for h in range(HALVES)]
+        for h in range(HALVES):
+            nc.scalar.activation(out=p_dz[h][:], in_=p_sb[:, h * BANK:(h + 1) * BANK], func=ACT.Copy, scale=dz_k[:])
+            add_turned(h, p_dz[h][:], False, True)
+        for h in range(HALVES):
+            cols = slice(h * BANK, (h + 1) * BANK)
+            vt = tile(f"vt{h}", [P, BLOCKS, P], F32)
+            nc.scalar.copy(out=vt[:], in_=vt_bank[h][:])
+            v_bank = bank(f"c{h}", f"v_bank{h}", [P, BANK])
+            for b in range(BLOCKS):
+                nc.tensor.transpose(v_bank[:, b * P:(b + 1) * P], vt[:, b, :], ident[:])
+            y = tile(f"y{h}", [P, BANK], F32)
+            nc.vector.scalar_tensor_tensor(out=y[:], in0=s1[:, cols], scalar=GRAD_SCALE, in1=v_bank[:],
+                                           op0=ALU.mult, op1=ALU.add)
+            nc.sync.dma_start(out=out[:, cols], in_=y[:])

@@ -22,8 +22,9 @@ PACK = 4
 BANK = 512
 HALVES = T // BANK
 BLOCKS = BANK // P
-KQ = 256
+KEY_CHUNKS = ((0, 512), (512, 768), (768, 1024))
 SH = I // 2
+OUT_RANGES = ((0, 256), (256, 640), (640, 1024))
 GRAD_SCALE = 1024.0
 
 
@@ -63,33 +64,34 @@ def tile_attend_bvaluepatch_kernel(tc, query, keys, gout, cvals_words, cvals_sca
         ident = tile("ident", [P, P], F32)
         make_identity(nc, ident[:])
         s1 = tile("s1", [P, T], F32)
-        nc.gpsimd.memset(s1[:], 0.0)
+        nc.vector.memset(s1[:], 0.0)
 
         q_raw = tile("q_raw", [P, PACK, Q], F32)
         nc.sync.dma_start(out=q_raw[:], in_=query.rearrange("(p t) q -> p t q", t=PACK))
-        keys_v = keys.rearrange("(p t) n -> p t n", t=PACK)
-        k_raw = [tile(f"k_raw{h}", [P, PACK, BANK], F32) for h in range(HALVES)]
-        for h in range(HALVES):
-            nc.sync.dma_start(out=k_raw[h][:], in_=keys_v[:, :, h * BANK:(h + 1) * BANK])
-        us_col = tile("us_col", [P, PACK], F32)
-        nc.scalar.dma_start(out=us_col[:], in_=us.rearrange("o (p j) -> (o p) j", j=PACK))
         for g in range(4):
-            nc.scalar.dma_start(out=cv_scales[32 * g:32 * g + 4, :].bitcast(I32),
-                                in_=cvals_scales[0][4 * g:4 * g + 4, :].bitcast(I32))
-        nc.sync.dma_start(idx[:], offs)
+            nc.sync.dma_start(out=cv_scales[32 * g:32 * g + 4, :].bitcast(I32),
+                              in_=cvals_scales[0][4 * g:4 * g + 4, :].bitcast(I32))
+        keys_v = keys.rearrange("(p t) n -> p t n", t=PACK)
+        k_raw = [tile(f"k_raw{c}", [P, PACK, hi - lo], F32) for c, (lo, hi) in enumerate(KEY_CHUNKS)]
+        for c, (lo, hi) in enumerate(KEY_CHUNKS):
+            nc.sync.dma_start(out=k_raw[c][:], in_=keys_v[:, :, lo:hi])
         nc.sync.dma_start(idx2[:], offs2)
+        nc.sync.dma_start(idx[:], offs)
         g_raw = tile("g_raw", [P, PACK, Q], F32)
         nc.sync.dma_start(out=g_raw[:], in_=gout.rearrange("(p t) q -> p t q", t=PACK))
+        corr_v = corr.rearrange("(p t) u -> p t u", t=PACK)
+        plane = [tile(f"plane{t}", [P, U], F32) for t in range(PACK)]
+        nc.sync.dma_start(out=plane[0][:], in_=corr_v[:, 0, :])
         cv_codes = tile("cv_codes", [P, T], U32)
         nc.sync.dma_start(out=cv_codes[:].bitcast(I32),
                           in_=cvals_words[0].rearrange("p n t -> p (n t)").bitcast(I32))
-        corr_v = corr.rearrange("(p t) u -> p t u", t=PACK)
-        plane = [tile(f"plane{t}", [P, U], F32) for t in range(PACK)]
-        for t in range(PACK):
+        us_col = tile("us_col", [P, PACK], F32)
+        nc.sync.dma_start(out=us_col[:], in_=us.rearrange("o (p j) -> (o p) j", j=PACK))
+        for t in range(1, PACK):
             nc.sync.dma_start(out=plane[t][:], in_=corr_v[:, t, :])
-        old_sb = [tile(f"old{h}", [P, BANK], F32) for h in range(HALVES)]
-        for h in range(HALVES):
-            nc.sync.dma_start(out=old_sb[h][:], in_=old[:, h * BANK:(h + 1) * BANK])
+        old_sb = [tile(f"old{r}", [P, hi - lo], F32) for r, (lo, hi) in enumerate(OUT_RANGES)]
+        for r, (lo, hi) in enumerate(OUT_RANGES):
+            nc.sync.dma_start(out=old_sb[r][:], in_=old[:, lo:hi])
 
         q_w = tile("q_w", [P, Q, PACK], BF16)
         dst, src = weave_views(q_raw[:], q_w[:])
@@ -103,25 +105,27 @@ def tile_attend_bvaluepatch_kernel(tc, query, keys, gout, cvals_words, cvals_sca
             nc.tensor.transpose(us_bank[:, j, :], us_col[:, j:j + 1].to_broadcast([P, P]), ident[:])
 
         a_sb = tile("a_sb", [P, T], F32)
-        neg_max = [tile(f"neg_max{h}", [P, 1], F32) for h in range(HALVES)]
-        for h in range(HALVES):
-            k_codes = tile(f"k_codes{h}", [P, BANK], U32)
-            k_scales = tile(f"k_scales{h}", [P, BANK], U8)
-            k_w = [tile(f"k_w{h}_{s}", [P, KQ, PACK], BF16) for s in range(2)]
-            for s in range(2):
-                dst, src = weave_views(k_raw[h][:, :, s * KQ:(s + 1) * KQ], k_w[s][:])
-                if s == 0:
-                    nc.vector.tensor_copy(out=dst, in_=src)
-                else:
-                    nc.scalar.activation(out=dst, in_=src, func=ACT.Copy)
-            for s in range(2):
-                quantize(nc, k_w[s][:], k_codes[:, s * KQ:(s + 1) * KQ], k_scales[:, s * KQ:(s + 1) * KQ])
-            a_bank = bank(f"a{h}", f"a_bank{h}", [P, BANK])
+        row_max = None
+        for c, (lo, hi) in enumerate(KEY_CHUNKS):
+            width = hi - lo
+            cut = width * 5 // 8
+            k_codes = tile(f"k_codes{c}", [P, width], U32)
+            k_scales = tile(f"k_scales{c}", [P, width], U8)
+            k_w = tile(f"k_w{c}", [P, width, PACK], BF16)
+            dst, src = weave_views(k_raw[c][:, :, :cut], k_w[:, :cut, :])
+            nc.vector.tensor_copy(out=dst, in_=src)
+            dst, src = weave_views(k_raw[c][:, :, cut:], k_w[:, cut:, :])
+            nc.scalar.activation(out=dst, in_=src, func=ACT.Copy)
+            quantize(nc, k_w[:], k_codes[:], k_scales[:])
+            a_bank = bank(f"a{c}", f"a_bank{c}", [P, width])
             mx(nc, a_bank[:], q_codes[:], q_scales[:], k_codes[:], k_scales[:])
-            nc.vector.tensor_reduce(out=neg_max[h][:], in_=a_bank[:], axis=AX.X, op=ALU.max, negate=True)
-            nc.scalar.copy(out=a_sb[:, h * BANK:(h + 1) * BANK], in_=a_bank[:])
+            new_max = tile(f"row_max{c}", [P, 1], F32)
+            nc.vector.tensor_scalar(out=a_sb[:, lo:hi], in0=a_bank[:], scalar1=1.0,
+                                    scalar2=None if row_max is None else row_max[:],
+                                    op0=ALU.mult, op1=ALU.max, accum_out=new_max[:])
+            row_max = new_max
         neg_m1 = tile("neg_m1", [P, 1], F32)
-        nc.vector.tensor_tensor(out=neg_m1[:], in0=neg_max[0][:], in1=neg_max[1][:], op=ALU.min)
+        nc.scalar.activation(out=neg_m1[:], in_=row_max[:], func=ACT.Copy, scale=-1.0)
 
         p_sb = tile("p_sb", [P, T], F32)
         z = tile("z", [P, 1], F32)
@@ -176,21 +180,22 @@ def tile_attend_bvaluepatch_kernel(tc, query, keys, gout, cvals_words, cvals_sca
         dz_b = tile("dz_b", [P, 1], F32)
         nc.scalar.activation(out=dz_b[:], in_=pc0_sum[1][:], func=ACT.Identity, scale=neg_rz[:], bias=dz_a[:])
 
-        vt_bank = [bank(f"a{h}", f"vt_bank{h}", [P, BLOCKS, P]) for h in range(HALVES)]
+        turned = range(1, len(OUT_RANGES))
+        vt_bank = {r: bank(f"a{r - 1}", f"vt_bank{r}", [P, OUT_RANGES[r][1] - OUT_RANGES[r][0]]) for r in turned}
 
-        def add_turned(h, src_ap, first, last):
-            for b in range(BLOCKS):
-                nc.tensor.matmul(vt_bank[h][:, b, :], lhsT=src_ap[:, b * P:(b + 1) * P], rhs=ident[:], is_transpose=True,
-                                 start=(first and b == 0), stop=(last and b == BLOCKS - 1))
+        def add_turned(r, src_ap, first, last):
+            blocks = src_ap.shape[1] // P
+            for b in range(blocks):
+                cols = slice(b * P, (b + 1) * P)
+                nc.tensor.matmul(vt_bank[r][:, cols], lhsT=src_ap[:, cols], rhs=ident[:], is_transpose=True,
+                                 start=(first and b == 0), stop=(last and b == blocks - 1))
 
-        for h in range(HALVES):
-            add_turned(h, pc0[:, h * BANK:(h + 1) * BANK], True, False)
+        for r in turned:
+            add_turned(r, pc0[:, OUT_RANGES[r][0]:OUT_RANGES[r][1]], True, False)
 
         for t in range(2, PACK):
             for s in range(2):
                 nc.vector.tensor_copy(c_w[s][:, :, t], plane[t][:].indirect(idx2[:, s * (SH // 16):(s + 1) * (SH // 16)]))
-        for h in range(HALVES):
-            add_turned(h, old_sb[h][:], False, False)
 
         c_codes = [tile(f"c_codes{s}", [P, SH], U32) for s in range(2)]
         c_scales = [tile(f"c_scales{s}", [P, SH], U8) for s in range(2)]
@@ -198,6 +203,11 @@ def tile_attend_bvaluepatch_kernel(tc, query, keys, gout, cvals_words, cvals_sca
         for s in range(2):
             quantize(nc, c_w[s][:], c_codes[s][:], c_scales[s][:])
             mx(nc, c1_bank[s][:], g_codes[:], g_scales[:], c_codes[s][:], c_scales[s][:])
+        for r in turned:
+            add_turned(r, old_sb[r][:], False, False)
+        lo, hi = OUT_RANGES[0]
+        base = tile("base", [P, hi - lo], F32)
+        nc.vector.tensor_tensor(out=base[:], in0=pc0[:, lo:hi], in1=old_sb[0][:], op=ALU.add)
 
         e1 = tile("e1", [P, I], F32)
         e1_sum = [tile(f"e1_sum{s}", [P, 1], F32) for s in range(2)]
@@ -212,18 +222,26 @@ def tile_attend_bvaluepatch_kernel(tc, query, keys, gout, cvals_words, cvals_sca
         dz_k = tile("dz_k", [P, 1], F32)
         nc.scalar.activation(out=dz_k[:], in_=e1_sum[1][:], func=ACT.Identity, scale=neg_rz_k[:], bias=dz_c[:])
 
-        p_dz = [tile(f"p_dz{h}", [P, BANK], F32) for h in range(HALVES)]
-        for h in range(HALVES):
-            nc.scalar.activation(out=p_dz[h][:], in_=p_sb[:, h * BANK:(h + 1) * BANK], func=ACT.Copy, scale=dz_k[:])
-            add_turned(h, p_dz[h][:], False, True)
-        for h in range(HALVES):
-            cols = slice(h * BANK, (h + 1) * BANK)
-            vt = tile(f"vt{h}", [P, BLOCKS, P], F32)
-            nc.scalar.copy(out=vt[:], in_=vt_bank[h][:])
-            v_bank = bank(f"c{h}", f"v_bank{h}", [P, BANK])
-            for b in range(BLOCKS):
-                nc.tensor.transpose(v_bank[:, b * P:(b + 1) * P], vt[:, b, :], ident[:])
-            y = tile(f"y{h}", [P, BANK], F32)
-            nc.vector.scalar_tensor_tensor(out=y[:], in0=s1[:, cols], scalar=GRAD_SCALE, in1=v_bank[:],
+        dense = {}
+        for r in turned:
+            lo, hi = OUT_RANGES[r]
+            p_dz = tile(f"p_dz{r}", [P, hi - lo], F32)
+            nc.scalar.activation(out=p_dz[:], in_=p_sb[:, lo:hi], func=ACT.Copy, scale=dz_k[:])
+            add_turned(r, p_dz[:], False, True)
+        for r in turned:
+            lo, hi = OUT_RANGES[r]
+            vt = tile(f"vt{r}", [P, hi - lo], F32)
+            nc.scalar.copy(out=vt[:], in_=vt_bank[r][:])
+            dense[r] = bank(f"c{r - 1}", f"v_bank{r}", [P, hi - lo])
+            for b in range((hi - lo) // P):
+                cols = slice(b * P, (b + 1) * P)
+                nc.tensor.transpose(dense[r][:, cols], vt[:, cols], ident[:])
+        lo, hi = OUT_RANGES[0]
+        dense[0] = tile("dense0", [P, hi - lo], F32)
+        nc.vector.scalar_tensor_tensor(out=dense[0][:], in0=p_sb[:, lo:hi], scalar=dz_k[:], in1=base[:],
+                                       op0=ALU.mult, op1=ALU.add)
+        for r, (lo, hi) in enumerate(OUT_RANGES):
+            y = tile(f"y{r}", [P, hi - lo], F32)
+            nc.vector.scalar_tensor_tensor(out=y[:], in0=s1[:, lo:hi], scalar=GRAD_SCALE, in1=dense[r][:],
                                            op0=ALU.mult, op1=ALU.add)
-            nc.sync.dma_start(out=out[:, cols], in_=y[:])
+            nc.sync.dma_start(out=out[:, lo:hi], in_=y[:])

@@ -24,7 +24,7 @@ HALVES = T // BANK
 BLOCKS = BANK // P
 KEY_CHUNKS = ((0, 512), (512, 768), (768, 1024))
 SH = I // 2
-OUT_RANGES = ((0, 256), (256, 640), (640, 1024))
+OUT_RANGES = ((0, 128), (128, 640), (640, 1024))
 GRAD_SCALE = 1024.0
 
 
@@ -50,8 +50,8 @@ def tile_attend_bvaluepatch_kernel(tc, query, keys, gout, cvals_words, cvals_sca
         sb = ctx.enter_context(tc.tile_pool(name="sb", bufs=1))
         ps = ctx.enter_context(tc.psum_pool(name="ps", bufs=1))
 
-        def tile(name, shape, dtype):
-            return sb.tile(shape, dtype, name=name, align_bytes=64)
+        def tile(name, shape, dtype, tag=None):
+            return sb.tile(shape, dtype, name=name, tag=tag or name, align_bytes=64)
 
         def bank(tag, name, shape):
             return ps.tile(shape, F32, name=name, tag=tag)
@@ -68,8 +68,10 @@ def tile_attend_bvaluepatch_kernel(tc, query, keys, gout, cvals_words, cvals_sca
 
         q_raw = tile("q_raw", [P, PACK, Q], F32)
         nc.sync.dma_start(out=q_raw[:], in_=query.rearrange("(p t) q -> p t q", t=PACK))
+        us_col = tile("us_col", [P, PACK], F32)
+        nc.scalar.dma_start(out=us_col[:], in_=us.rearrange("o (p j) -> (o p) j", j=PACK))
         for g in range(4):
-            nc.sync.dma_start(out=cv_scales[32 * g:32 * g + 4, :].bitcast(I32),
+            nc.scalar.dma_start(out=cv_scales[32 * g:32 * g + 4, :].bitcast(I32),
                               in_=cvals_scales[0][4 * g:4 * g + 4, :].bitcast(I32))
         keys_v = keys.rearrange("(p t) n -> p t n", t=PACK)
         k_raw = [tile(f"k_raw{c}", [P, PACK, hi - lo], F32) for c, (lo, hi) in enumerate(KEY_CHUNKS)]
@@ -85,8 +87,6 @@ def tile_attend_bvaluepatch_kernel(tc, query, keys, gout, cvals_words, cvals_sca
         cv_codes = tile("cv_codes", [P, T], U32)
         nc.sync.dma_start(out=cv_codes[:].bitcast(I32),
                           in_=cvals_words[0].rearrange("p n t -> p (n t)").bitcast(I32))
-        us_col = tile("us_col", [P, PACK], F32)
-        nc.sync.dma_start(out=us_col[:], in_=us.rearrange("o (p j) -> (o p) j", j=PACK))
         for t in range(1, PACK):
             nc.sync.dma_start(out=plane[t][:], in_=corr_v[:, t, :])
         old_sb = [tile(f"old{r}", [P, hi - lo], F32) for r, (lo, hi) in enumerate(OUT_RANGES)]
@@ -105,25 +105,39 @@ def tile_attend_bvaluepatch_kernel(tc, query, keys, gout, cvals_words, cvals_sca
             nc.tensor.transpose(us_bank[:, j, :], us_col[:, j:j + 1].to_broadcast([P, P]), ident[:])
 
         a_sb = tile("a_sb", [P, T], F32)
-        row_max = None
-        for c, (lo, hi) in enumerate(KEY_CHUNKS):
-            width = hi - lo
-            cut = width * 5 // 8
+        k_w, a_bank = [], []
+
+        def score(c):
+            width = k_w[c].shape[1]
             k_codes = tile(f"k_codes{c}", [P, width], U32)
             k_scales = tile(f"k_scales{c}", [P, width], U8)
-            k_w = tile(f"k_w{c}", [P, width, PACK], BF16)
-            dst, src = weave_views(k_raw[c][:, :, :cut], k_w[:, :cut, :])
+            quantize(nc, k_w[c][:], k_codes[:], k_scales[:])
+            a_bank.append(bank(f"a{c}", f"a_bank{c}", [P, width]))
+            mx(nc, a_bank[c][:], q_codes[:], q_scales[:], k_codes[:], k_scales[:])
+
+        for c, (lo, hi) in enumerate(KEY_CHUNKS):
+            cut = (hi - lo) // 2
+            k_w.append(tile(f"k_w{c}", [P, hi - lo, PACK], BF16))
+            dst, src = weave_views(k_raw[c][:, :, :cut], k_w[c][:, :cut, :])
             nc.vector.tensor_copy(out=dst, in_=src)
-            dst, src = weave_views(k_raw[c][:, :, cut:], k_w[:, cut:, :])
+            dst, src = weave_views(k_raw[c][:, :, cut:], k_w[c][:, cut:, :])
             nc.scalar.activation(out=dst, in_=src, func=ACT.Copy)
-            quantize(nc, k_w[:], k_codes[:], k_scales[:])
-            a_bank = bank(f"a{c}", f"a_bank{c}", [P, width])
-            mx(nc, a_bank[:], q_codes[:], q_scales[:], k_codes[:], k_scales[:])
+            if c > 0:
+                score(c - 1)
+        score(len(KEY_CHUNKS) - 1)
+        g_w = tile("g_w", [P, Q, PACK], BF16)
+        dst, src = weave_views(g_raw[:], g_w[:])
+        nc.scalar.activation(out=dst, in_=src, func=ACT.Copy)
+        row_max = None
+        for c, (lo, hi) in enumerate(KEY_CHUNKS):
             new_max = tile(f"row_max{c}", [P, 1], F32)
-            nc.vector.tensor_scalar(out=a_sb[:, lo:hi], in0=a_bank[:], scalar1=1.0,
+            nc.vector.tensor_scalar(out=a_sb[:, lo:hi], in0=a_bank[c][:], scalar1=1.0,
                                     scalar2=None if row_max is None else row_max[:],
                                     op0=ALU.mult, op1=ALU.max, accum_out=new_max[:])
             row_max = new_max
+        g_codes = tile("g_codes", [P, Q], U32)
+        g_scales = tile("g_scales", [P, Q], U8)
+        quantize(nc, g_w[:], g_codes[:], g_scales[:])
         neg_m1 = tile("neg_m1", [P, 1], F32)
         nc.scalar.activation(out=neg_m1[:], in_=row_max[:], func=ACT.Copy, scale=-1.0)
 
@@ -131,54 +145,47 @@ def tile_attend_bvaluepatch_kernel(tc, query, keys, gout, cvals_words, cvals_sca
         z = tile("z", [P, 1], F32)
         nc.scalar.activation(out=p_sb[:], in_=a_sb[:], func=ACT.Exp, bias=neg_m1[:], accum_out=z[:])
 
-        g_w = tile("g_w", [P, Q, PACK], BF16)
-        dst, src = weave_views(g_raw[:], g_w[:])
-        nc.scalar.activation(out=dst, in_=src, func=ACT.Copy)
-        g_codes = tile("g_codes", [P, Q], U32)
-        g_scales = tile("g_scales", [P, Q], U8)
-        quantize(nc, g_w[:], g_codes[:], g_scales[:])
-        c0_bank = [bank(f"c{h}", f"c0_bank{h}", [P, BANK]) for h in range(HALVES)]
-        for h in range(HALVES):
-            cols = slice(h * BANK, (h + 1) * BANK)
-            mx(nc, c0_bank[h][:], g_codes[:], g_scales[:], cv_codes[:, cols], cv_scales[:, cols])
-
+        c_w = [tile(f"c_w{s}", [P, SH, PACK], BF16) for s in range(2)]
+        pair = tile("pair", [P, 2, I], BF16)
         ax = tile("ax", [P, I], F32)
         nc.vector.tensor_copy(ax[:], a_sb[:].indirect(idx[:]))
         px = tile("px", [P, I], F32)
         nc.scalar.activation(out=px[:], in_=ax[:], func=ACT.Exp, bias=neg_m1[:])
+        nc.vector.tensor_copy(pair[:, 0, :], plane[0][:].indirect(idx2[:]))
+
 
         rz = tile("rz", [P, 1], F32)
         nc.vector.reciprocal(out=rz[:], in_=z[:])
+        c0_bank = [bank(f"c{h}", f"c0_bank{h}", [P, BANK]) for h in range(HALVES)]
+        for h in range(HALVES):
+            cols = slice(h * BANK, (h + 1) * BANK)
+            mx(nc, c0_bank[h][:], g_codes[:], g_scales[:], cv_codes[:, cols], cv_scales[:, cols])
         rz_k = tile("rz_k", [P, 1], F32)
         nc.vector.tensor_scalar(out=rz_k[:], in0=rz[:], scalar1=GRAD_SCALE, scalar2=None, op0=ALU.mult)
-        neg_rz_k = tile("neg_rz_k", [P, 1], F32)
-        nc.scalar.activation(out=neg_rz_k[:], in_=rz[:], func=ACT.Copy, scale=-GRAD_SCALE)
-        neg_rz = tile("neg_rz", [P, 1], F32)
-        nc.scalar.activation(out=neg_rz[:], in_=rz[:], func=ACT.Copy, scale=-1.0)
-
-        c_w = [tile(f"c_w{s}", [P, SH, PACK], BF16) for s in range(2)]
-        pair = tile("pair", [P, 2, I], BF16)
-        nc.vector.tensor_copy(pair[:, 0, :], plane[0][:].indirect(idx2[:]))
-
         pc0 = tile("pc0", [P, T], F32)
         pc0_sum = [tile(f"pc0_sum{h}", [P, 1], F32) for h in range(HALVES)]
         for h in range(HALVES):
             cols = slice(h * BANK, (h + 1) * BANK)
             nc.vector.scalar_tensor_tensor(out=pc0[:, cols], in0=c0_bank[h][:], scalar=rz_k[:], in1=p_sb[:, cols],
                                            op0=ALU.mult, op1=ALU.mult, accum_out=pc0_sum[h][:])
+
         nc.vector.tensor_copy(pair[:, 1, :], plane[1][:].indirect(idx2[:]))
-        w = tile("w", [P, I], F32)
+        w = tile("w", [P, I], F32, tag="plane1")
         nc.vector.scalar_tensor_tensor(out=w[:].rearrange("p (n j) -> p n j", j=PACK),
                                        in0=px[:].rearrange("p (n j) -> p n j", j=PACK), scalar=rz[:],
                                        in1=us_bank[:].rearrange("p j n -> p n j"), op0=ALU.mult, op1=ALU.mult)
-        for s in range(2):
-            nc.scalar.copy(out=c_w[s][:, :, 0:2],
-                           in_=pair[:, :, s * SH:(s + 1) * SH].rearrange("p t n -> p n t"))
-
+        neg_rz_k = tile("neg_rz_k", [P, 1], F32)
+        nc.scalar.activation(out=neg_rz_k[:], in_=rz[:], func=ACT.Copy, scale=-GRAD_SCALE)
+        neg_rz = tile("neg_rz", [P, 1], F32)
+        nc.scalar.activation(out=neg_rz[:], in_=rz[:], func=ACT.Copy, scale=-1.0)
         dz_a = tile("dz_a", [P, 1], F32)
         nc.scalar.activation(out=dz_a[:], in_=pc0_sum[0][:], func=ACT.Copy, scale=neg_rz[:])
         dz_b = tile("dz_b", [P, 1], F32)
         nc.scalar.activation(out=dz_b[:], in_=pc0_sum[1][:], func=ACT.Identity, scale=neg_rz[:], bias=dz_a[:])
+
+        for s in range(2):
+            nc.scalar.copy(out=c_w[s][:, :, 0:2],
+                           in_=pair[:, :, s * SH:(s + 1) * SH].rearrange("p t n -> p n t"))
 
         turned = range(1, len(OUT_RANGES))
         vt_bank = {r: bank(f"a{r - 1}", f"vt_bank{r}", [P, OUT_RANGES[r][1] - OUT_RANGES[r][0]]) for r in turned}

@@ -24,7 +24,7 @@ HALVES = T // BANK
 BLOCKS = BANK // P
 KEY_CHUNKS = ((0, 512), (512, 768), (768, 1024))
 SH = I // 2
-OUT_RANGES = ((0, 128), (128, 640), (640, 1024))
+OUT_RANGES = ((0, 256), (256, 640), (640, 1024))
 GRAD_SCALE = 1024.0
 
 
@@ -68,19 +68,20 @@ def tile_attend_bvaluepatch_kernel(tc, query, keys, gout, cvals_words, cvals_sca
 
         q_raw = tile("q_raw", [P, PACK, Q], F32)
         nc.sync.dma_start(out=q_raw[:], in_=query.rearrange("(p t) q -> p t q", t=PACK))
-        us_col = tile("us_col", [P, PACK], F32)
-        nc.scalar.dma_start(out=us_col[:], in_=us.rearrange("o (p j) -> (o p) j", j=PACK))
+        scale_rows = tile("scale_rows", [P, T // 4], I32)
         for g in range(4):
-            nc.scalar.dma_start(out=cv_scales[32 * g:32 * g + 4, :].bitcast(I32),
-                              in_=cvals_scales[0][4 * g:4 * g + 4, :].bitcast(I32))
+            nc.sync.dma_start(out=scale_rows[32 * g:32 * g + 4, :],
+                                in_=cvals_scales[0][4 * g:4 * g + 4, :].bitcast(I32))
+        us_col = tile("us_col", [P, PACK], F32)
+        nc.sync.dma_start(out=us_col[:], in_=us.rearrange("o (p j) -> (o p) j", j=PACK))
         keys_v = keys.rearrange("(p t) n -> p t n", t=PACK)
         k_raw = [tile(f"k_raw{c}", [P, PACK, hi - lo], F32) for c, (lo, hi) in enumerate(KEY_CHUNKS)]
         for c, (lo, hi) in enumerate(KEY_CHUNKS):
             nc.sync.dma_start(out=k_raw[c][:], in_=keys_v[:, :, lo:hi])
-        nc.sync.dma_start(idx2[:], offs2)
-        nc.sync.dma_start(idx[:], offs)
         g_raw = tile("g_raw", [P, PACK, Q], F32)
         nc.sync.dma_start(out=g_raw[:], in_=gout.rearrange("(p t) q -> p t q", t=PACK))
+        nc.sync.dma_start(idx2[:], offs2)
+        nc.sync.dma_start(idx[:], offs)
         corr_v = corr.rearrange("(p t) u -> p t u", t=PACK)
         plane = [tile(f"plane{t}", [P, U], F32) for t in range(PACK)]
         nc.sync.dma_start(out=plane[0][:], in_=corr_v[:, 0, :])
@@ -103,6 +104,9 @@ def tile_attend_bvaluepatch_kernel(tc, query, keys, gout, cvals_words, cvals_sca
         us_bank = bank("us", "us_bank", [P, PACK, P])
         for j in range(PACK):
             nc.tensor.transpose(us_bank[:, j, :], us_col[:, j:j + 1].to_broadcast([P, P]), ident[:])
+
+        us_row = tile("us_row", [P, I], F32)
+        nc.scalar.copy(out=us_row[:].rearrange("p (n j) -> p n j", j=PACK), in_=us_bank[:].rearrange("p j n -> p n j"))
 
         a_sb = tile("a_sb", [P, T], F32)
         k_w, a_bank = [], []
@@ -152,28 +156,32 @@ def tile_attend_bvaluepatch_kernel(tc, query, keys, gout, cvals_words, cvals_sca
         px = tile("px", [P, I], F32)
         nc.scalar.activation(out=px[:], in_=ax[:], func=ACT.Exp, bias=neg_m1[:])
         nc.vector.tensor_copy(pair[:, 0, :], plane[0][:].indirect(idx2[:]))
+        w = tile("w", [P, I], F32, tag="plane0")
+        nc.gpsimd.tensor_tensor(out=w[:], in0=px[:], in1=us_row[:], op=ALU.mult)
 
 
         rz = tile("rz", [P, 1], F32)
         nc.vector.reciprocal(out=rz[:], in_=z[:])
+        for g in range(4):
+            rows = slice(32 * g, 32 * g + 4)
+            nc.vector.tensor_copy(out=cv_scales[rows, :].bitcast(I32), in_=scale_rows[rows, :])
         c0_bank = [bank(f"c{h}", f"c0_bank{h}", [P, BANK]) for h in range(HALVES)]
         for h in range(HALVES):
             cols = slice(h * BANK, (h + 1) * BANK)
             mx(nc, c0_bank[h][:], g_codes[:], g_scales[:], cv_codes[:, cols], cv_scales[:, cols])
         rz_k = tile("rz_k", [P, 1], F32)
-        nc.vector.tensor_scalar(out=rz_k[:], in0=rz[:], scalar1=GRAD_SCALE, scalar2=None, op0=ALU.mult)
-        pc0 = tile("pc0", [P, T], F32)
+        nc.scalar.activation(out=rz_k[:], in_=rz[:], func=ACT.Copy, scale=GRAD_SCALE)
         pc0_sum = [tile(f"pc0_sum{h}", [P, 1], F32) for h in range(HALVES)]
-        for h in range(HALVES):
-            cols = slice(h * BANK, (h + 1) * BANK)
-            nc.vector.scalar_tensor_tensor(out=pc0[:, cols], in0=c0_bank[h][:], scalar=rz_k[:], in1=p_sb[:, cols],
+
+        def weigh_c0(h, dst_ap):
+            nc.vector.scalar_tensor_tensor(out=dst_ap, in0=c0_bank[h][:], scalar=rz_k[:],
+                                           in1=p_sb[:, h * BANK:(h + 1) * BANK],
                                            op0=ALU.mult, op1=ALU.mult, accum_out=pc0_sum[h][:])
 
+        pc0 = [tile(f"pc0_{h}", [P, BANK], F32) for h in range(HALVES)]
+        for h in range(HALVES):
+            weigh_c0(h, pc0[h][:])
         nc.vector.tensor_copy(pair[:, 1, :], plane[1][:].indirect(idx2[:]))
-        w = tile("w", [P, I], F32, tag="plane1")
-        nc.vector.scalar_tensor_tensor(out=w[:].rearrange("p (n j) -> p n j", j=PACK),
-                                       in0=px[:].rearrange("p (n j) -> p n j", j=PACK), scalar=rz[:],
-                                       in1=us_bank[:].rearrange("p j n -> p n j"), op0=ALU.mult, op1=ALU.mult)
         neg_rz_k = tile("neg_rz_k", [P, 1], F32)
         nc.scalar.activation(out=neg_rz_k[:], in_=rz[:], func=ACT.Copy, scale=-GRAD_SCALE)
         neg_rz = tile("neg_rz", [P, 1], F32)
@@ -190,15 +198,17 @@ def tile_attend_bvaluepatch_kernel(tc, query, keys, gout, cvals_words, cvals_sca
         turned = range(1, len(OUT_RANGES))
         vt_bank = {r: bank(f"a{r - 1}", f"vt_bank{r}", [P, OUT_RANGES[r][1] - OUT_RANGES[r][0]]) for r in turned}
 
-        def add_turned(r, src_ap, first, last):
-            blocks = src_ap.shape[1] // P
-            for b in range(blocks):
-                cols = slice(b * P, (b + 1) * P)
-                nc.tensor.matmul(vt_bank[r][:, cols], lhsT=src_ap[:, cols], rhs=ident[:], is_transpose=True,
-                                 start=(first and b == 0), stop=(last and b == blocks - 1))
+        def blocks_of(ap):
+            return [ap[:, c:c + P] for c in range(0, ap.shape[1], P)]
 
+        def add_turned(r, blocks, first, last):
+            for b, block in enumerate(blocks):
+                nc.tensor.matmul(vt_bank[r][:, b * P:(b + 1) * P], lhsT=block, rhs=ident[:], is_transpose=True,
+                                 start=(first and b == 0), stop=(last and b == len(blocks) - 1))
+
+        pc0_blocks = blocks_of(pc0[0][:]) + blocks_of(pc0[1][:])
         for r in turned:
-            add_turned(r, pc0[:, OUT_RANGES[r][0]:OUT_RANGES[r][1]], True, False)
+            add_turned(r, pc0_blocks[OUT_RANGES[r][0] // P:OUT_RANGES[r][1] // P], True, False)
 
         for t in range(2, PACK):
             for s in range(2):
@@ -211,16 +221,16 @@ def tile_attend_bvaluepatch_kernel(tc, query, keys, gout, cvals_words, cvals_sca
             quantize(nc, c_w[s][:], c_codes[s][:], c_scales[s][:])
             mx(nc, c1_bank[s][:], g_codes[:], g_scales[:], c_codes[s][:], c_scales[s][:])
         for r in turned:
-            add_turned(r, old_sb[r][:], False, False)
+            add_turned(r, blocks_of(old_sb[r][:]), False, False)
         lo, hi = OUT_RANGES[0]
         base = tile("base", [P, hi - lo], F32)
-        nc.vector.tensor_tensor(out=base[:], in0=pc0[:, lo:hi], in1=old_sb[0][:], op=ALU.add)
+        nc.vector.tensor_tensor(out=base[:], in0=pc0[0][:, lo:hi], in1=old_sb[0][:], op=ALU.add)
 
         e1 = tile("e1", [P, I], F32)
         e1_sum = [tile(f"e1_sum{s}", [P, 1], F32) for s in range(2)]
         for s in range(2):
             cols = slice(s * SH, (s + 1) * SH)
-            nc.vector.scalar_tensor_tensor(out=e1[:, cols], in0=c1_bank[s][:], scalar=1.0, in1=w[:, cols],
+            nc.vector.scalar_tensor_tensor(out=e1[:, cols], in0=c1_bank[s][:], scalar=rz[:], in1=w[:, cols],
                                            op0=ALU.mult, op1=ALU.mult, accum_out=e1_sum[s][:])
         nc.vector.tensor_copy(s1[:].indirect(idx[:]), e1[:])
 
@@ -234,7 +244,7 @@ def tile_attend_bvaluepatch_kernel(tc, query, keys, gout, cvals_words, cvals_sca
             lo, hi = OUT_RANGES[r]
             p_dz = tile(f"p_dz{r}", [P, hi - lo], F32)
             nc.scalar.activation(out=p_dz[:], in_=p_sb[:, lo:hi], func=ACT.Copy, scale=dz_k[:])
-            add_turned(r, p_dz[:], False, True)
+            add_turned(r, blocks_of(p_dz[:]), False, True)
         for r in turned:
             lo, hi = OUT_RANGES[r]
             vt = tile(f"vt{r}", [P, hi - lo], F32)

from contextlib import ExitStack

import concourse.mybir as mybir
from concourse.masks import make_identity

D, E, T, I, U, Q = 512, 512, 1024, 512, 2048, 128
FLOPS = 2 * Q * (D * T + E * T + E * I)

F32 = mybir.dt.float32
BF16 = mybir.dt.bfloat16
I32 = mybir.dt.int32
U32 = mybir.dt.uint32
U16 = mybir.dt.uint16
U8 = mybir.dt.uint8
FP8X4 = mybir.dt.float8_e4m3fn_x4
ALU = mybir.AluOpType
ACT = mybir.ActivationFunctionType
AX = mybir.AxisListType

P = 128
PACK = 4
BANK = 512
HALVES = T // BANK
BLOCKS = BANK // P
KEY_CHUNKS = ((0, 512), (512, 768), (768, 1024))
SH = I // 2
OUT_RANGES = ((0, 256), (256, 640), (640, 1024))
GRAD_SCALE = 1024.0


def weave_views(raw, woven):
    return (
        woven.rearrange("p (c i) t -> p c t i", i=4),
        raw.rearrange("p t (c i) -> p c t i", i=4),
    )


def quantize(nc, woven, codes, scales):
    nc.vector.quantize_mx(out=codes.bitcast(FP8X4), scales=scales, in_=woven.rearrange("p w t -> p (w t)"))


def mx(nc, out, lhs, lhs_scales, rhs, rhs_scales):
    nc.tensor.matmul_mx(out=out, lhsT=lhs.bitcast(FP8X4), lhsT_scale=lhs_scales,
                        rhs=rhs.bitcast(FP8X4), rhs_scale=rhs_scales, start=True, stop=True)


def tile_attend_bvaluepatch_kernel(tc, query, keys, gout, cvals_words, cvals_scales, corr, us, old, offs, offs2, out):
    nc = tc.nc
    with ExitStack() as ctx:
        sb = ctx.enter_context(tc.tile_pool(name="sb", bufs=1))
        ps = ctx.enter_context(tc.psum_pool(name="ps", bufs=1))

        def tile(name, shape, dtype, tag=None):
            return sb.tile(shape, dtype, name=name, tag=tag or name, align_bytes=64)

        def bank(tag, name, shape):
            return ps.tile(shape, F32, name=name, tag=tag)

        idx = sb.tile([P, I // 16], U16, name="idx")
        idx2 = sb.tile([P, I // 16], U16, name="idx2")

        cv_scales = tile("cv_scales", [P, T], U8)
        nc.gpsimd.memset(cv_scales[:].bitcast(U32), 0)
        ident = tile("ident", [P, P], F32)
        make_identity(nc, ident[:])
        s1 = tile("s1", [P, T], F32)
        nc.vector.memset(s1[:], 0.0)

        q_raw = tile("q_raw", [P, PACK, Q], F32)
        nc.sync.dma_start(out=q_raw[:], in_=query.rearrange("(p t) q -> p t q", t=PACK))
        scale_rows = tile("scale_rows", [P, T // 4], I32)
        for g in range(4):
            nc.sync.dma_start(out=scale_rows[32 * g:32 * g + 4, :],
                                in_=cvals_scales[0][4 * g:4 * g + 4, :].bitcast(I32))
        us_col = tile("us_col", [P, PACK], F32)
        nc.sync.dma_start(out=us_col[:], in_=us.rearrange("o (p j) -> (o p) j", j=PACK))
        keys_v = keys.rearrange("(p t) n -> p t n", t=PACK)
        k_raw = [tile(f"k_raw{c}", [P, PACK, hi - lo], F32) for c, (lo, hi) in enumerate(KEY_CHUNKS)]
        for c, (lo, hi) in enumerate(KEY_CHUNKS):
            nc.sync.dma_start(out=k_raw[c][:], in_=keys_v[:, :, lo:hi])
        g_raw = tile("g_raw", [P, PACK, Q], F32)
        nc.sync.dma_start(out=g_raw[:], in_=gout.rearrange("(p t) q -> p t q", t=PACK))
        nc.sync.dma_start(idx2[:], offs2)
        nc.sync.dma_start(idx[:], offs)
        corr_v = corr.rearrange("(p t) u -> p t u", t=PACK)
        plane = [tile(f"plane{t}", [P, U], F32) for t in range(PACK)]
        nc.sync.dma_start(out=plane[0][:], in_=corr_v[:, 0, :])
        cv_codes = tile("cv_codes", [P, T], U32)
        nc.sync.dma_start(out=cv_codes[:].bitcast(I32),
                          in_=cvals_words[0].rearrange("p n t -> p (n t)").bitcast(I32))
        for t in range(1, PACK):
            nc.sync.dma_start(out=plane[t][:], in_=corr_v[:, t, :])
        old_sb = [tile(f"old{r}", [P, hi - lo], F32) for r, (lo, hi) in enumerate(OUT_RANGES)]
        for r, (lo, hi) in enumerate(OUT_RANGES):
            nc.sync.dma_start(out=old_sb[r][:], in_=old[:, lo:hi])

        q_w = tile("q_w", [P, Q, PACK], BF16)
        dst, src = weave_views(q_raw[:], q_w[:])
        nc.scalar.activation(out=dst, in_=src, func=ACT.Copy)
        q_codes = tile("q_codes", [P, Q], U32)
        q_scales = tile("q_scales", [P, Q], U8)
        quantize(nc, q_w[:], q_codes[:], q_scales[:])

        us_bank = bank("us", "us_bank", [P, PACK, P])
        for j in range(PACK):
            nc.tensor.transpose(us_bank[:, j, :], us_col[:, j:j + 1].to_broadcast([P, P]), ident[:])

        us_row = tile("us_row", [P, I], F32)
        nc.scalar.copy(out=us_row[:].rearrange("p (n j) -> p n j", j=PACK), in_=us_bank[:].rearrange("p j n -> p n j"))

        a_sb = tile("a_sb", [P, T], F32)
        k_w, a_bank = [], []

        def score(c):
            width = k_w[c].shape[1]
            k_codes = tile(f"k_codes{c}", [P, width], U32)
            k_scales = tile(f"k_scales{c}", [P, width], U8)
            quantize(nc, k_w[c][:], k_codes[:], k_scales[:])
            a_bank.append(bank(f"a{c}", f"a_bank{c}", [P, width]))
            mx(nc, a_bank[c][:], q_codes[:], q_scales[:], k_codes[:], k_scales[:])

        for c, (lo, hi) in enumerate(KEY_CHUNKS):
            cut = (hi - lo) // 2
            k_w.append(tile(f"k_w{c}", [P, hi - lo, PACK], BF16))
            dst, src = weave_views(k_raw[c][:, :, :cut], k_w[c][:, :cut, :])
            nc.vector.tensor_copy(out=dst, in_=src)
            dst, src = weave_views(k_raw[c][:, :, cut:], k_w[c][:, cut:, :])
            nc.scalar.activation(out=dst, in_=src, func=ACT.Copy)
            if c > 0:
                score(c - 1)
        score(len(KEY_CHUNKS) - 1)
        g_w = tile("g_w", [P, Q, PACK], BF16)
        dst, src = weave_views(g_raw[:], g_w[:])
        nc.scalar.activation(out=dst, in_=src, func=ACT.Copy)
        row_max = None
        for c, (lo, hi) in enumerate(KEY_CHUNKS):
            new_max = tile(f"row_max{c}", [P, 1], F32)
            nc.vector.tensor_scalar(out=a_sb[:, lo:hi], in0=a_bank[c][:], scalar1=1.0,
                                    scalar2=None if row_max is None else row_max[:],
                                    op0=ALU.mult, op1=ALU.max, accum_out=new_max[:])
            row_max = new_max
        g_codes = tile("g_codes", [P, Q], U32)
        g_scales = tile("g_scales", [P, Q], U8)
        quantize(nc, g_w[:], g_codes[:], g_scales[:])
        neg_m1 = tile("neg_m1", [P, 1], F32)
        nc.scalar.activation(out=neg_m1[:], in_=row_max[:], func=ACT.Copy, scale=-1.0)

        p_sb = tile("p_sb", [P, T], F32)
        z = tile("z", [P, 1], F32)
        nc.scalar.activation(out=p_sb[:], in_=a_sb[:], func=ACT.Exp, bias=neg_m1[:], accum_out=z[:])

        c_w = [tile(f"c_w{s}", [P, SH, PACK], BF16) for s in range(2)]
        pair = tile("pair", [P, 2, I], BF16)
        ax = tile("ax", [P, I], F32)
        nc.vector.tensor_copy(ax[:], a_sb[:].indirect(idx[:]))
        px = tile("px", [P, I], F32)
        nc.scalar.activation(out=px[:], in_=ax[:], func=ACT.Exp, bias=neg_m1[:])
        nc.vector.tensor_copy(pair[:, 0, :], plane[0][:].indirect(idx2[:]))
        w = tile("w", [P, I], F32, tag="plane0")
        nc.gpsimd.tensor_tensor(out=w[:], in0=px[:], in1=us_row[:], op=ALU.mult)


        rz = tile("rz", [P, 1], F32)
        nc.vector.reciprocal(out=rz[:], in_=z[:])
        for g in range(4):
            rows = slice(32 * g, 32 * g + 4)
            nc.vector.tensor_copy(out=cv_scales[rows, :].bitcast(I32), in_=scale_rows[rows, :])
        c0_bank = [bank(f"c{h}", f"c0_bank{h}", [P, BANK]) for h in range(HALVES)]
        for h in range(HALVES):
            cols = slice(h * BANK, (h + 1) * BANK)
            mx(nc, c0_bank[h][:], g_codes[:], g_scales[:], cv_codes[:, cols], cv_scales[:, cols])
        rz_k = tile("rz_k", [P, 1], F32)
        nc.scalar.activation(out=rz_k[:], in_=rz[:], func=ACT.Copy, scale=GRAD_SCALE)
        pc0_sum = [tile(f"pc0_sum{h}", [P, 1], F32) for h in range(HALVES)]

        def weigh_c0(h, dst_ap):
            nc.vector.scalar_tensor_tensor(out=dst_ap, in0=c0_bank[h][:], scalar=rz_k[:],
                                           in1=p_sb[:, h * BANK:(h + 1) * BANK],
                                           op0=ALU.mult, op1=ALU.mult, accum_out=pc0_sum[h][:])

        pc0 = [tile(f"pc0_{h}", [P, BANK], F32) for h in range(HALVES)]
        for h in range(HALVES):
            weigh_c0(h, pc0[h][:])
        nc.vector.tensor_copy(pair[:, 1, :], plane[1][:].indirect(idx2[:]))
        neg_rz_k = tile("neg_rz_k", [P, 1], F32)
        nc.scalar.activation(out=neg_rz_k[:], in_=rz[:], func=ACT.Copy, scale=-GRAD_SCALE)
        neg_rz = tile("neg_rz", [P, 1], F32)
        nc.scalar.activation(out=neg_rz[:], in_=rz[:], func=ACT.Copy, scale=-1.0)
        dz_a = tile("dz_a", [P, 1], F32)
        nc.scalar.activation(out=dz_a[:], in_=pc0_sum[0][:], func=ACT.Copy, scale=neg_rz[:])
        dz_b = tile("dz_b", [P, 1], F32)
        nc.scalar.activation(out=dz_b[:], in_=pc0_sum[1][:], func=ACT.Identity, scale=neg_rz[:], bias=dz_a[:])

        for s in range(2):
            nc.scalar.copy(out=c_w[s][:, :, 0:2],
                           in_=pair[:, :, s * SH:(s + 1) * SH].rearrange("p t n -> p n t"))

        turned = range(1, len(OUT_RANGES))
        vt_bank = {r: bank(f"a{r - 1}", f"vt_bank{r}", [P, OUT_RANGES[r][1] - OUT_RANGES[r][0]]) for r in turned}

        def blocks_of(ap):
            return [ap[:, c:c + P] for c in range(0, ap.shape[1], P)]

        def add_turned(r, blocks, first, last):
            for b, block in enumerate(blocks):
                nc.tensor.matmul(vt_bank[r][:, b * P:(b + 1) * P], lhsT=block, rhs=ident[:], is_transpose=True,
                                 start=(first and b == 0), stop=(last and b == len(blocks) - 1))

        pc0_blocks = blocks_of(pc0[0][:]) + blocks_of(pc0[1][:])
        for r in turned:
            add_turned(r, pc0_blocks[OUT_RANGES[r][0] // P:OUT_RANGES[r][1] // P], True, False)

        for t in range(2, PACK):
            for s in range(2):
                nc.vector.tensor_copy(c_w[s][:, :, t], plane[t][:].indirect(idx2[:, s * (SH // 16):(s + 1) * (SH // 16)]))

        c_codes = [tile(f"c_codes{s}", [P, SH], U32) for s in range(2)]
        c_scales = [tile(f"c_scales{s}", [P, SH], U8) for s in range(2)]
        c1_bank = [bank(f"e{s}", f"c1_bank{s}", [P, SH]) for s in range(2)]
        for s in range(2):
            quantize(nc, c_w[s][:], c_codes[s][:], c_scales[s][:])
            mx(nc, c1_bank[s][:], g_codes[:], g_scales[:], c_codes[s][:], c_scales[s][:])
        for r in turned:
            add_turned(r, blocks_of(old_sb[r][:]), False, False)
        lo, hi = OUT_RANGES[0]
        base = tile("base", [P, hi - lo], F32)
        nc.vector.tensor_tensor(out=base[:], in0=pc0[0][:, lo:hi], in1=old_sb[0][:], op=ALU.add)

        e1 = tile("e1", [P, I], F32)
        e1_sum = [tile(f"e1_sum{s}", [P, 1], F32) for s in range(2)]
        for s in range(2):
            cols = slice(s * SH, (s + 1) * SH)
            nc.vector.scalar_tensor_tensor(out=e1[:, cols], in0=c1_bank[s][:], scalar=rz[:], in1=w[:, cols],
                                           op0=ALU.mult, op1=ALU.mult, accum_out=e1_sum[s][:])
        nc.vector.tensor_copy(s1[:].indirect(idx[:]), e1[:])

        dz_c = tile("dz_c", [P, 1], F32)
        nc.scalar.activation(out=dz_c[:], in_=e1_sum[0][:], func=ACT.Identity, scale=neg_rz_k[:], bias=dz_b[:])
        dz_k = tile("dz_k", [P, 1], F32)
        nc.scalar.activation(out=dz_k[:], in_=e1_sum[1][:], func=ACT.Identity, scale=neg_rz_k[:], bias=dz_c[:])

        dense = {}
        for r in turned:
            lo, hi = OUT_RANGES[r]
            p_dz = tile(f"p_dz{r}", [P, hi - lo], F32)
            nc.scalar.activation(out=p_dz[:], in_=p_sb[:, lo:hi], func=ACT.Copy, scale=dz_k[:])
            add_turned(r, blocks_of(p_dz[:]), False, True)
        for r in turned:
            lo, hi = OUT_RANGES[r]
            vt = tile(f"vt{r}", [P, hi - lo], F32)
            nc.scalar.copy(out=vt[:], in_=vt_bank[r][:])
            dense[r] = bank(f"c{r - 1}", f"v_bank{r}", [P, hi - lo])
            for b in range((hi - lo) // P):
                cols = slice(b * P, (b + 1) * P)
                nc.tensor.transpose(dense[r][:, cols], vt[:, cols], ident[:])
        lo, hi = OUT_RANGES[0]
        dense[0] = tile("dense0", [P, hi - lo], F32)
        nc.vector.scalar_tensor_tensor(out=dense[0][:], in0=p_sb[:, lo:hi], scalar=dz_k[:], in1=base[:],
                                       op0=ALU.mult, op1=ALU.add)
        for r, (lo, hi) in enumerate(OUT_RANGES):
            y = tile(f"y{r}", [P, hi - lo], F32)
            nc.vector.scalar_tensor_tensor(out=y[:], in0=s1[:, lo:hi], scalar=GRAD_SCALE, in1=dense[r][:],
                                           op0=ALU.mult, op1=ALU.add)
            nc.sync.dma_start(out=out[:, lo:hi], in_=y[:])
